import numpy as np
import ml_dtypes


def mxq(x, axis, fmt="e4m3"):
    dtype, down = {"e4m3": (ml_dtypes.float8_e4m3fn, 7), "e5m2": (ml_dtypes.float8_e5m2, 14)}[fmt]
    v = np.moveaxis(np.asarray(x, np.float32).astype(ml_dtypes.bfloat16).astype(np.float64), axis, -1)
    blocks = v.reshape(v.shape[:-1] + (-1, 32))
    amax = np.abs(blocks).max(-1, keepdims=True)
    byte = np.maximum(np.where(amax > 0, np.frexp(amax)[1] - 1 + 127, 0) - down, 1)
    scale = np.exp2(byte - 127.0)
    codes = (blocks / scale).astype(np.float32).astype(dtype).astype(np.float64)
    return np.moveaxis((codes * scale).reshape(v.shape), -1, axis)


WIDE = False


def mx_kscale(k):
    if not WIDE:
        return np.ones(k)
    levels = np.array([10, -10, 5, -5, 0])
    if k % 512:
        return np.exp2(np.random.permutation(np.resize(levels, k // 32))).repeat(32)
    a = np.empty((k // 512, 16))
    for p in range(k // 512):
        a[p, :8] = np.random.permutation(np.resize(levels, 8))
        for g in range(8):
            far = levels[np.abs(levels - a[p, g]) >= 10]
            a[p, g + 8] = far[np.random.randint(len(far))]
    return np.exp2(a.ravel()).repeat(32)


def f64(x):
    return np.asarray(x).astype(np.float64)


def striped(idx):
    return np.tile(idx.reshape(-1, 16).T, (8, 1)).astype(np.uint16)


def unstriped(offs):
    return offs[:16].T.reshape(-1).astype(np.int64)


E2M1 = np.array([0.0, 0.5, 1.0, 1.5, 2.0, 3.0, 4.0, 6.0, -0.0, -0.5, -1.0, -1.5, -2.0, -3.0, -4.0, -6.0])


def pack_weight(w, fmt):
    k, n = w.shape
    w = f64(np.asarray(w, np.float32).astype(ml_dtypes.bfloat16)).reshape(k // 32, 32, n)
    amax = np.abs(w).max(1)
    if fmt == "e4m3":
        byte = np.frexp(amax)[1] - 1 + 127 - 7
    else:
        mant, ex = np.frexp(amax / 6.0)
        byte = np.where(mant > 0.5, ex, ex - 1) + 127
    byte = np.clip(np.where(amax > 0, byte, 1), 1, 254)
    scaled = (w * np.exp2(127.0 - byte)[:, None, :]).reshape(k, n).astype(np.float32)
    by_word = np.ascontiguousarray(scaled.reshape(k // 512, 128, 4, n).transpose(0, 1, 3, 2))
    if fmt == "e4m3":
        words = by_word.astype(ml_dtypes.float8_e4m3fn).view(np.uint8)
    else:
        c = by_word.astype(ml_dtypes.float4_e2m1fn).view(np.uint8) & 0xF
        words = (c[..., 0::2] | (c[..., 1::2] << 4)).reshape(k // 512, 128, 2 * n)
    return np.ascontiguousarray(words), np.ascontiguousarray(byte.astype(np.uint8).reshape(k // 512, 16, n))


def unpack_weight(words, scales, fmt):
    g, _, n = scales.shape
    words = np.ascontiguousarray(words).reshape(g, 128, n, -1)
    if fmt == "e4m3":
        vals = words.view(ml_dtypes.float8_e4m3fn).astype(np.float64)
    else:
        nib = np.empty((g, 128, n, 4), np.uint8)
        nib[..., 0::2] = words & 0xF
        nib[..., 1::2] = words >> 4
        vals = E2M1[nib]
    vals = vals * np.repeat(np.exp2(scales.astype(np.float64) - 127.0), 8, axis=1)[..., None]
    return vals.transpose(0, 1, 3, 2).reshape(g * 512, n)


def gelu(v):
    return 0.5 * v * (1.0 + np.tanh(np.sqrt(2.0 / np.pi) * (v + 0.044715 * v**3)))


K, T, S, S2 = 1024, 2048, 512, 1024


def setup_inputs():
    n = np.random.standard_normal
    s = mx_kscale(K)[:, None]
    d = {}
    d["tab_words"], d["tab_scales"] = pack_weight(n((K, T)) * s, "e4m3")
    d["offs"] = striped(np.random.permutation(T)[:S])
    d["offs2"] = striped(np.random.permutation(T)[:S2])
    d["w1"] = (n((K, K)) / s / s.T / K).astype(np.float32)
    d["w4_words"], d["w4_scales"] = pack_weight(n((K, K)) / s / K ** 0.5, "e2m1")
    d["wf_words"], d["wf_scales"] = pack_weight(n((K, S)) / s / K ** 0.5, "e4m3")
    d["gain"] = (np.exp(0.4 * n(K)) / s[:, 0] / K ** 0.5).astype(np.float32)
    d["gv"] = (1.2 * np.exp(0.4 * n(S2))).astype(np.float32)
    return d


def reference(tab_words, tab_scales, offs, offs2, w1, w4_words, w4_scales,
              wf_words, wf_scales, gain, gv):
    TW = unpack_weight(tab_words, tab_scales, "e4m3")
    v = TW[:, unstriped(offs)]
    v2 = TW[:, unstriped(offs2)]
    w4 = unpack_weight(w4_words, w4_scales, "e2m1")
    wf = unpack_weight(wf_words, wf_scales, "e4m3")
    h = np.abs(mxq(f64(w1), 0, "e4m3").T @ v)
    hq = mxq(h, 0, "e4m3")
    b = f64(gain)[:, None] * (w4.T @ v)
    bq = mxq(b, 0, "e4m3")
    e = f64(gv)[:, None] * (v2.T @ hq)
    f = v2.T @ bq + v2.T @ wf
    x = np.maximum(e, f)
    return 0.5 * x * (1.0 + np.tanh(0.7978845608028654 * (x + 0.044715 * x ** 3)))

@@ -1,0 +1,269 @@
+from contextlib import ExitStack
+
+import concourse.mybir as mybir
+
+K, T, S, S2 = 1024, 2048, 512, 1024
+FLOPS = 2 * K * K * S * 2 + 2 * K * S2 * S * 3
+
+F32 = mybir.dt.float32
+BF16 = mybir.dt.bfloat16
+I32 = mybir.dt.int32
+U32 = mybir.dt.uint32
+U16 = mybir.dt.uint16
+U8 = mybir.dt.uint8
+FP8X4 = mybir.dt.float8_e4m3fn_x4
+FP4X4 = mybir.dt.float4_e2m1fn_x4
+ACT = mybir.ActivationFunctionType
+ALU = mybir.AluOpType
+
+P = 128
+PASSES = 2
+SLOTS = 4
+CH = 128
+NCH = S // CH
+MT = S2 // P
+RES_SLICE = 512
+
+
+def tile_list_turnout_companions_kernel(tc, tab_words, tab_scales, offs, offs2, w1, w4_words, w4_scales,
+                                                  wf_words, wf_scales, gain, gv, out):
+    nc = tc.nc
+    with ExitStack() as ctx:
+        keep = ctx.enter_context(tc.tile_pool(name="keep", bufs=1))
+        ring = ctx.enter_context(tc.tile_pool(name="ring", bufs=4))
+        shared = ctx.enter_context(tc.tile_pool(name="shared", bufs=1))
+        psum = ctx.enter_context(tc.psum_pool(name="psum", bufs=4))
+
+        def held(name, shape, dtype, tag=""):
+            return keep.tile(shape, dtype, name=name, tag=tag or name, align_bytes=64)
+
+        offs_sb = keep.tile([P, S // 16], U16, name="offs_sb")
+        offs2_sb = keep.tile([P, S2 // 16], U16, name="offs2_sb")
+        tab_sc = held("tab_sc", [P, T], U8)
+        w4_raw = held("w4_raw", [P, PASSES * 2 * K], U8)
+        w4_sc_raw = shared.tile([P, PASSES * K], U8, name="w4_sc_raw", align_bytes=64, offset=16384 - 64)
+        wf_sc = held("wf_sc", [P, S], U8)
+        gain_sb = held("gain_sb", [P, PASSES * SLOTS], F32)
+        v_sc1 = held("v_sc1", [P, S], U8)
+        warm_in = held("warm_in", [P, 8], F32)
+        warm_out = held("warm_out", [P, 8], F32)
+
+        nc.vector.memset(tab_sc[:].bitcast(I32), 0)
+        nc.vector.memset(warm_in[:], 0.0)
+        nc.vector.memset(w4_sc_raw[:].bitcast(I32), 0)
+        nc.gpsimd.memset(v_sc1[:].bitcast(I32), 0)
+
+        nc.sync.dma_start(offs_sb[:], offs)
+        for q in range(4):
+            nc.scalar.dma_start(out=tab_sc[32 * q : 32 * q + 8, :].bitcast(I32),
+                                in_=tab_scales[:, 4 * q : 4 * q + 4, :].bitcast(I32))
+        nc.scalar.activation(warm_out[:], warm_in[:], ACT.Gelu_apprx_tanh)
+        for q in range(4):
+            nc.scalar.dma_start(
+                out=w4_sc_raw[32 * q : 32 * q + 4, :].bitcast(I32).rearrange("r (a c) -> r a c", a=PASSES),
+                in_=w4_scales[:, 4 * q : 4 * q + 4, :].bitcast(I32).rearrange("a r c -> r a c"))
+        nc.gpsimd.dma_start(out=gain_sb[:].rearrange("p (b t) -> p b t", t=SLOTS),
+                            in_=gain.rearrange("(b p t) -> p b t", p=P, t=SLOTS))
+        nc.gpsimd.memset(wf_sc[:].bitcast(I32), 0)
+        for q in range(4):
+            nc.gpsimd.dma_start(out=wf_sc[32 * q : 32 * q + 8, :].bitcast(I32),
+                                in_=wf_scales[:, 4 * q : 4 * q + 4, :].bitcast(I32))
+
+        tab_w = [held("tab_w0", [P, T], U32), held("tab_w1", [P, T], U32, tag="warm_in")]
+        w1_raw = [held("w1_raw0", [P, PASSES * 2048], F32, tag="warm_out")]
+
+        def load_w1(a, b, u):
+            c0 = 512 * b + 256 * u
+            nc.sync.dma_start(
+                out=w1_raw[b][:, 2048 * a + 1024 * u : 2048 * a + 1024 * (u + 1)].rearrange("p (j c) -> p j c", j=SLOTS),
+                in_=w1[512 * a : 512 * (a + 1), c0 : c0 + 256].rearrange("(p j) c -> p j c", j=SLOTS))
+
+        def load_tab(a):
+            nc.sync.dma_start(out=tab_w[a][:].bitcast(I32),
+                              in_=tab_words[a].rearrange("p t i -> p (t i)").bitcast(I32))
+
+        nc.sync.dma_start(out=w4_raw[:].bitcast(I32).rearrange("p (a c) -> p a c", a=PASSES),
+                          in_=w4_words.bitcast(I32).rearrange("a p c -> p a c"))
+        load_tab(0)
+        nc.sync.dma_start(offs2_sb[:], offs2)
+        load_w1(0, 0, 0)
+        load_tab(1)
+        load_w1(0, 0, 1)
+        load_w1(1, 0, 0)
+        load_w1(1, 0, 1)
+
+        v_sc = held("v_sc", [P, S], U8)
+        v_w = [held("v_w%d" % a, [P, S], U32) for a in range(PASSES)]
+        w4_w = [held("w4_w%d" % a, [P, 2 * K], U8) for a in range(PASSES)]
+        w4_sc = held("w4_sc", [P, PASSES * K], U8)
+
+        def deal_words(a):
+            nc.vector.tensor_copy(
+                out=w4_w[a][:].bitcast(U16).rearrange("p (t o i) -> p o t i", t=SLOTS, i=8),
+                in_=w4_raw[:, 2 * K * a : 2 * K * (a + 1)].bitcast(U16).rearrange("p (o i t) -> p o t i", t=SLOTS, i=8))
+
+        def deal_scales(a):
+            nc.vector.tensor_copy(
+                out=w4_sc[:, K * a : K * (a + 1)].rearrange("p (t o i) -> p o t i", t=SLOTS, i=16),
+                in_=w4_sc_raw[:, K * a : K * (a + 1)].rearrange("p (o i t) -> p o t i", t=SLOTS, i=16))
+
+        nc.vector.tensor_copy(v_sc[:], tab_sc[:].indirect(offs_sb[:]))
+        for q in range(4):
+            nc.scalar.dma_start(out=v_sc1[32 * q : 32 * q + 4, :].bitcast(I32),
+                                in_=v_sc[32 * q + 4 : 32 * q + 8, :].bitcast(I32))
+        deal_words(0)
+        nc.vector.tensor_copy(v_w[0][:], tab_w[0][:].indirect(offs_sb[:]))
+        deal_scales(0)
+        nc.vector.tensor_copy(v_w[1][:], tab_w[1][:].indirect(offs_sb[:]))
+        deal_words(1)
+        deal_scales(1)
+
+        wf_w = held("wf_w", [P, PASSES * S], U32, tag="w4_raw")
+        nc.sync.dma_start(out=wf_w[:].bitcast(I32).rearrange("p (a c) -> p a c", a=PASSES),
+                          in_=wf_words.rearrange("a p c i -> p a (c i)").bitcast(I32))
+        w1_raw.append(shared.tile([P, PASSES * 2048], F32, name="w1_raw1", align_bytes=64, offset=0))
+        for a in range(PASSES):
+            for u in range(2):
+                load_w1(a, 1, u)
+
+        r_sc = {}
+        r_w = {}
+
+        def gather_residents(s, scales, words):
+            cols = offs2_sb[:, s * RES_SLICE // 16 : (s + 1) * RES_SLICE // 16]
+            r_sc[s] = scales
+            nc.vector.tensor_copy(r_sc[s][:], tab_sc[:].indirect(cols))
+            for a in range(PASSES):
+                r_w[a, s] = words[a]
+                nc.vector.tensor_copy(r_w[a, s][:], tab_w[a][:].indirect(cols))
+
+        def quantize_halves(name, grouped):
+            codes = held(name + "_w", [P, S], U32)
+            scales = held(name + "_sc", [P, S], U8)
+            for u in range(2):
+                nc.vector.quantize_mx(out=codes[:, 256 * u : 256 * (u + 1)].bitcast(FP8X4),
+                                      scales=scales[:, 256 * u : 256 * (u + 1)],
+                                      in_=grouped[:, 1024 * u : 1024 * (u + 1)])
+            return codes, scales
+
+        def w4_pass(dst, a, b, t, cols, start, stop):
+            col = 256 * t + P * b
+            plane = v_sc if a == 0 else v_sc1
+            nc.tensor.matmul_mx(
+                out=dst,
+                lhsT=w4_w[a][:, 2 * col : 2 * (col + P)].bitcast(FP4X4),
+                lhsT_scale=w4_sc[:, K * a + col : K * a + col + P],
+                rhs=v_w[a][:, cols].bitcast(FP8X4), rhs_scale=plane[:, cols], start=start, stop=stop)
+
+        def b_block_vector(b):
+            grouped = held("b_g%d" % b, [P, S * SLOTS], BF16)
+            banks = [psum.tile([P, SLOTS, CH], F32, name="first", tag="first") for c in range(NCH)]
+            for c in range(NCH):
+                for a in range(PASSES):
+                    for t in range(SLOTS):
+                        w4_pass(banks[c][:, t, :], a, b, t, slice(CH * c, CH * (c + 1)),
+                                a == 0 and t == 0, a == PASSES - 1 and t == SLOTS - 1)
+                nc.vector.tensor_tensor(
+                    out=grouped[:, SLOTS * CH * c : SLOTS * CH * (c + 1)].rearrange("p (n t) -> p n t", t=SLOTS),
+                    in0=banks[c][:].rearrange("p t n -> p n t"),
+                    in1=gain_sb[:, SLOTS * b : SLOTS * (b + 1)].unsqueeze(1).to_broadcast([P, CH, SLOTS]),
+                    op=ALU.mult)
+            return quantize_halves("bq%d" % b, grouped)
+
+        def b_block_scalar(b):
+            flat = held("b_flat%d" % b, [P, SLOTS * S], BF16)
+            grouped = held("b_g%d" % b, [P, S * SLOTS], BF16)
+            banks = [psum.tile([P, S], F32, name="first", tag="first") for t in range(SLOTS)]
+            for a in range(PASSES):
+                for t in range(SLOTS):
+                    w4_pass(banks[t][:], a, b, t, slice(0, S), a == 0, a == PASSES - 1)
+            for t in range(SLOTS):
+                nc.scalar.activation(out=flat[:, S * t : S * (t + 1)], in_=banks[t][:], func=ACT.Copy,
+                                     scale=gain_sb[:, SLOTS * b + t : SLOTS * b + t + 1])
+            for u in range(2):
+                nc.vector.tensor_copy(
+                    out=grouped[:, 1024 * u : 1024 * (u + 1)].rearrange("p (c i t) -> p c t i", t=SLOTS, i=4),
+                    in_=flat[:].rearrange("p (t c i) -> p c t i", t=SLOTS, i=4)[:, 64 * u : 64 * (u + 1)])
+            return quantize_halves("bq%d" % b, grouped)
+
+        bq = [b_block_scalar(0), b_block_vector(1)]
+        gv_sb = held("gv_sb", [P, MT], F32, tag="w4_w0")
+        with nc.allow_non_contiguous_dma(reason="one factor a partition"):
+            nc.sync.dma_start(out=gv_sb[:], in_=gv.rearrange("(mt p) -> p mt", p=P))
+
+        def h_block(b):
+            w1q = []
+            for a in range(PASSES):
+                grouped = held("w1_g%d%d" % (a, b), [P, 2048], BF16)
+                for u in range(2):
+                    raw = w1_raw[b][:, 2048 * a + 1024 * u : 2048 * a + 1024 * (u + 1)]
+                    nc.scalar.copy(
+                        out=grouped[:].rearrange("p (t m j) -> p m j t", t=SLOTS, j=SLOTS)[:, 64 * u : 64 * (u + 1)],
+                        in_=raw.rearrange("p (j m t) -> p m j t", t=SLOTS, j=SLOTS))
+                codes = held("w1_w%d%d" % (a, b), [P, 512], U32)
+                scales = held("w1_sc%d%d" % (a, b), [P, 512], U8)
+                nc.vector.quantize_mx(out=codes[:].bitcast(FP8X4), scales=scales[:], in_=grouped[:])
+                w1q.append((codes, scales))
+            grouped = held("h_g%d" % b, [P, S * SLOTS], BF16)
+            for c in range(NCH):
+                bank = psum.tile([P, SLOTS, CH], F32, name="first", tag="first")
+                for a in range(PASSES):
+                    for t in range(SLOTS):
+                        nc.tensor.matmul_mx(
+                            out=bank[:, t, :],
+                            lhsT=w1q[a][0][:, P * t : P * (t + 1)].bitcast(FP8X4),
+                            lhsT_scale=w1q[a][1][:, P * t : P * (t + 1)],
+                            rhs=v_w[a][:, CH * c : CH * (c + 1)].bitcast(FP8X4),
+                            rhs_scale=v_sc[4 * a : P, CH * c : CH * (c + 1)],
+                            start=(a == 0 and t == 0), stop=(a == PASSES - 1 and t == SLOTS - 1))
+                nc.scalar.activation(
+                    out=grouped[:, SLOTS * CH * c : SLOTS * CH * (c + 1)].rearrange("p (n t) -> p n t", t=SLOTS),
+                    in_=bank[:].rearrange("p t n -> p n t"), func=ACT.Abs)
+            return quantize_halves("hq%d" % b, grouped)
+
+        def resident_pass(bank, m, a, codes, scales, start, stop):
+            s, c0 = divmod(P * m, RES_SLICE)
+            nc.tensor.matmul_mx(
+                out=bank[:],
+                lhsT=r_w[a, s][:, c0 : c0 + P].bitcast(FP8X4),
+                lhsT_scale=r_sc[s][4 * a : P, c0 : c0 + P],
+                rhs=codes.bitcast(FP8X4), rhs_scale=scales, start=start, stop=stop)
+
+        f_sb = []
+
+        def f_tile(m):
+            bank = psum.tile([P, S], F32, name="second", tag="second")
+            for a in range(PASSES):
+                resident_pass(bank, m, a, wf_w[:, S * a : S * (a + 1)], wf_sc[4 * a : P, :], a == 0, False)
+            for a in range(PASSES):
+                resident_pass(bank, m, a, bq[a][0][:], bq[a][1][:], False, a == PASSES - 1)
+            f_m = held("f_sb%d" % m, [P, S], F32)
+            nc.scalar.copy(out=f_m[:], in_=bank[:])
+            f_sb.append(f_m)
+
+        def e_tile(m):
+            bank = psum.tile([P, S], F32, name="second", tag="second")
+            for a in range(PASSES):
+                resident_pass(bank, m, a, hq[a][0][:], hq[a][1][:], a == 0, a == PASSES - 1)
+            larger = ring.tile([P, S], F32, name="larger")
+            nc.vector.scalar_tensor_tensor(out=larger[:], in0=bank[:], scalar=gv_sb[:, m : m + 1], in1=f_sb[m][:],
+                                           op0=ALU.mult, op1=ALU.max)
+            result = ring.tile([P, S], F32, name="result")
+            nc.scalar.activation(out=result[:], in_=larger[:], func=ACT.Gelu_apprx_tanh)
+            nc.sync.dma_start(out=out[P * m : P * (m + 1), :], in_=result[:])
+
+        hq = [h_block(0)]
+        gather_residents(0, shared.tile([P, RES_SLICE], U8, name="r_sc0", align_bytes=64, offset=16384),
+                         [shared.tile([P, RES_SLICE], U32, name="r_w00", align_bytes=64, offset=16384 + 512),
+                          held("r_w10", [P, RES_SLICE], U32)])
+        for m in range(MT // 2):
+            f_tile(m)
+        hq.append(h_block(1))
+        gather_residents(1, held("r_sc1", [P, RES_SLICE], U8, tag="w1_g10"),
+                         [held("r_w01", [P, RES_SLICE], U32, tag="w1_g01"),
+                          held("r_w11", [P, RES_SLICE], U32, tag="w1_g11")])
+        for m in range(MT // 2):
+            e_tile(m)
+            f_tile(MT // 2 + m)
+        for m in range(MT // 2, MT):
+            e_tile(m)

@@ -23,6 +23,9 @@ CH = 128
 NCH = S // CH
 MT = S2 // P
 RES_SLICE = 512
+LEAD = 5
+HI = 2 * 8192
+LO = HI + 4096
 
 
 def tile_list_turnout_companions_kernel(tc, tab_words, tab_scales, offs, offs2, w1, w4_words, w4_scales,
@@ -41,42 +44,35 @@ def tile_list_turnout_companions_kernel(tc, tab_words, tab_scales, offs, offs2, 
         offs2_sb = keep.tile([P, S2 // 16], U16, name="offs2_sb")
         tab_sc = held("tab_sc", [P, T], U8)
         w4_raw = held("w4_raw", [P, PASSES * 2 * K], U8)
-        w4_sc_raw = shared.tile([P, PASSES * K], U8, name="w4_sc_raw", align_bytes=64, offset=16384 - 64)
         wf_sc = held("wf_sc", [P, S], U8)
-        gain_sb = held("gain_sb", [P, PASSES * SLOTS], F32)
         v_sc1 = held("v_sc1", [P, S], U8)
-        warm_in = held("warm_in", [P, 8], F32)
-        warm_out = held("warm_out", [P, 8], F32)
+        warm_in = shared.tile([P, 32], F32, name="warm_in", align_bytes=64, offset=LO + 16384 - 64)
+        warm_out = shared.tile([P, 192], F32, name="warm_out", align_bytes=64, offset=HI + 1920)
 
         nc.vector.memset(tab_sc[:].bitcast(I32), 0)
         nc.vector.memset(warm_in[:], 0.0)
-        nc.vector.memset(w4_sc_raw[:].bitcast(I32), 0)
         nc.gpsimd.memset(v_sc1[:].bitcast(I32), 0)
 
         nc.sync.dma_start(offs_sb[:], offs)
         for q in range(4):
             nc.scalar.dma_start(out=tab_sc[32 * q : 32 * q + 8, :].bitcast(I32),
                                 in_=tab_scales[:, 4 * q : 4 * q + 4, :].bitcast(I32))
-        nc.scalar.activation(warm_out[:], warm_in[:], ACT.Gelu_apprx_tanh)
-        for q in range(4):
-            nc.scalar.dma_start(
-                out=w4_sc_raw[32 * q : 32 * q + 4, :].bitcast(I32).rearrange("r (a c) -> r a c", a=PASSES),
-                in_=w4_scales[:, 4 * q : 4 * q + 4, :].bitcast(I32).rearrange("a r c -> r a c"))
-        nc.gpsimd.dma_start(out=gain_sb[:].rearrange("p (b t) -> p b t", t=SLOTS),
-                            in_=gain.rearrange("(b p t) -> p b t", p=P, t=SLOTS))
+        nc.scalar.activation(warm_out[:, 0:32], warm_in[:], ACT.Gelu_apprx_tanh)
         nc.gpsimd.memset(wf_sc[:].bitcast(I32), 0)
         for q in range(4):
             nc.gpsimd.dma_start(out=wf_sc[32 * q : 32 * q + 8, :].bitcast(I32),
                                 in_=wf_scales[:, 4 * q : 4 * q + 4, :].bitcast(I32))
 
-        tab_w = [held("tab_w0", [P, T], U32), held("tab_w1", [P, T], U32, tag="warm_in")]
-        w1_raw = [held("w1_raw0", [P, PASSES * 2048], F32, tag="warm_out")]
+        tab_w = [held("tab_w0", [P, T], U32), shared.tile([P, T], U32, name="tab_w1", align_bytes=64, offset=LO + 16384)]
+        w1_lo = shared.tile([P, 2 * 2048], F32, name="w1_lo", align_bytes=64, offset=LO)
+        w1_raw = {(a, 0): w1_lo[:, 2048 * a : 2048 * (a + 1)] for a in range(PASSES)}
+        gain_sb = shared.tile([P, PASSES * SLOTS], F32, name="gain_sb", align_bytes=64, offset=HI + 2560)
 
-        def load_w1(a, b, u):
-            c0 = 512 * b + 256 * u
+        def load_w1(a, b, u, width):
+            c0 = 512 * b + width * u
             nc.sync.dma_start(
-                out=w1_raw[b][:, 2048 * a + 1024 * u : 2048 * a + 1024 * (u + 1)].rearrange("p (j c) -> p j c", j=SLOTS),
-                in_=w1[512 * a : 512 * (a + 1), c0 : c0 + 256].rearrange("(p j) c -> p j c", j=SLOTS))
+                out=w1_raw[a, b].rearrange("p (j c) -> p j c", j=SLOTS)[:, :, width * u : width * (u + 1)],
+                in_=w1[512 * a : 512 * (a + 1), c0 : c0 + width].rearrange("(p j) c -> p j c", j=SLOTS))
 
         def load_tab(a):
             nc.sync.dma_start(out=tab_w[a][:].bitcast(I32),
@@ -86,11 +82,16 @@ def tile_list_turnout_companions_kernel(tc, tab_words, tab_scales, offs, offs2, 
                           in_=w4_words.bitcast(I32).rearrange("a p c -> p a c"))
         load_tab(0)
         nc.sync.dma_start(offs2_sb[:], offs2)
-        load_w1(0, 0, 0)
         load_tab(1)
-        load_w1(0, 0, 1)
-        load_w1(1, 0, 0)
-        load_w1(1, 0, 1)
+        load_w1(0, 0, 0, 512)
+        load_w1(1, 0, 0, 512)
+        nc.sync.dma_start(out=gain_sb[:].rearrange("p (b t) -> p b t", t=SLOTS),
+                          in_=gain.rearrange("(b p t) -> p b t", p=P, t=SLOTS))
+        w4_sc_raw = shared.tile([P, PASSES * K], U8, name="w4_sc_raw", align_bytes=64, offset=HI - 64)
+        nc.vector.memset(w4_sc_raw[:].bitcast(I32), 0)
+        for q in range(4):
+            nc.scalar.dma_start(out=w4_sc_raw[32 * q : 32 * q + 4, :].bitcast(I32),
+                                in_=w4_scales[:, 4 * q : 4 * q + 4, :].bitcast(I32).rearrange("a r c -> r a c"))
 
         v_sc = held("v_sc", [P, S], U8)
         v_w = [held("v_w%d" % a, [P, S], U32) for a in range(PASSES)]
@@ -109,7 +110,7 @@ def tile_list_turnout_companions_kernel(tc, tab_words, tab_scales, offs, offs2, 
 
         nc.vector.tensor_copy(v_sc[:], tab_sc[:].indirect(offs_sb[:]))
         for q in range(4):
-            nc.scalar.dma_start(out=v_sc1[32 * q : 32 * q + 4, :].bitcast(I32),
+            nc.gpsimd.dma_start(out=v_sc1[32 * q : 32 * q + 4, :].bitcast(I32),
                                 in_=v_sc[32 * q + 4 : 32 * q + 8, :].bitcast(I32))
         deal_words(0)
         nc.vector.tensor_copy(v_w[0][:], tab_w[0][:].indirect(offs_sb[:]))
@@ -121,10 +122,12 @@ def tile_list_turnout_companions_kernel(tc, tab_words, tab_scales, offs, offs2, 
         wf_w = held("wf_w", [P, PASSES * S], U32, tag="w4_raw")
         nc.sync.dma_start(out=wf_w[:].bitcast(I32).rearrange("p (a c) -> p a c", a=PASSES),
                           in_=wf_words.rearrange("a p c i -> p a (c i)").bitcast(I32))
-        w1_raw.append(shared.tile([P, PASSES * 2048], F32, name="w1_raw1", align_bytes=64, offset=0))
+        w1_hi = shared.tile([P, 2 * 2048], F32, name="w1_hi", align_bytes=64, offset=0)
         for a in range(PASSES):
-            for u in range(2):
-                load_w1(a, 1, u)
+            w1_raw[a, 1] = w1_hi[:, 2048 * a : 2048 * (a + 1)]
+        load_w1(0, 1, 0, 512)
+        load_w1(1, 1, 0, 256)
+        load_w1(1, 1, 1, 256)
 
         r_sc = {}
         r_w = {}
@@ -157,12 +160,13 @@ def tile_list_turnout_companions_kernel(tc, tab_words, tab_scales, offs, offs2, 
 
         def b_block_vector(b):
             grouped = held("b_g%d" % b, [P, S * SLOTS], BF16)
-            banks = [psum.tile([P, SLOTS, CH], F32, name="first", tag="first") for c in range(NCH)]
-            for c in range(NCH):
-                for a in range(PASSES):
+            banks = [psum.tile([P, SLOTS, CH], F32, name="second", tag="second") for c in range(NCH)]
+            for a in range(PASSES):
+                for c in range(NCH):
                     for t in range(SLOTS):
                         w4_pass(banks[c][:, t, :], a, b, t, slice(CH * c, CH * (c + 1)),
                                 a == 0 and t == 0, a == PASSES - 1 and t == SLOTS - 1)
+            for c in range(NCH):
                 nc.vector.tensor_tensor(
                     out=grouped[:, SLOTS * CH * c : SLOTS * CH * (c + 1)].rearrange("p (n t) -> p n t", t=SLOTS),
                     in0=banks[c][:].rearrange("p t n -> p n t"),
@@ -196,10 +200,10 @@ def tile_list_turnout_companions_kernel(tc, tab_words, tab_scales, offs, offs2, 
             for a in range(PASSES):
                 grouped = held("w1_g%d%d" % (a, b), [P, 2048], BF16)
                 for u in range(2):
-                    raw = w1_raw[b][:, 2048 * a + 1024 * u : 2048 * a + 1024 * (u + 1)]
-                    nc.scalar.copy(
+                    cast = nc.vector.tensor_copy if (b, u) == (1, 1) else nc.scalar.copy
+                    cast(
                         out=grouped[:].rearrange("p (t m j) -> p m j t", t=SLOTS, j=SLOTS)[:, 64 * u : 64 * (u + 1)],
-                        in_=raw.rearrange("p (j m t) -> p m j t", t=SLOTS, j=SLOTS))
+                        in_=w1_raw[a, b].rearrange("p (j m t) -> p m j t", t=SLOTS, j=SLOTS)[:, 64 * u : 64 * (u + 1)])
                 codes = held("w1_w%d%d" % (a, b), [P, 512], U32)
                 scales = held("w1_sc%d%d" % (a, b), [P, 512], U8)
                 nc.vector.quantize_mx(out=codes[:].bitcast(FP8X4), scales=scales[:], in_=grouped[:])
@@ -252,18 +256,15 @@ def tile_list_turnout_companions_kernel(tc, tab_words, tab_scales, offs, offs2, 
             nc.scalar.activation(out=result[:], in_=larger[:], func=ACT.Gelu_apprx_tanh)
             nc.sync.dma_start(out=out[P * m : P * (m + 1), :], in_=result[:])
 
-        hq = [h_block(0)]
-        gather_residents(0, shared.tile([P, RES_SLICE], U8, name="r_sc0", align_bytes=64, offset=16384),
-                         [shared.tile([P, RES_SLICE], U32, name="r_w00", align_bytes=64, offset=16384 + 512),
+        hq = [h_block(0), h_block(1)]
+        gather_residents(0, shared.tile([P, RES_SLICE], U8, name="r_sc0", align_bytes=64, offset=HI),
+                         [shared.tile([P, RES_SLICE], U32, name="r_w00", align_bytes=64, offset=HI + 512),
                           held("r_w10", [P, RES_SLICE], U32)])
-        for m in range(MT // 2):
-            f_tile(m)
-        hq.append(h_block(1))
         gather_residents(1, held("r_sc1", [P, RES_SLICE], U8, tag="w1_g10"),
                          [held("r_w01", [P, RES_SLICE], U32, tag="w1_g01"),
                           held("r_w11", [P, RES_SLICE], U32, tag="w1_g11")])
-        for m in range(MT // 2):
-            e_tile(m)
-            f_tile(MT // 2 + m)
-        for m in range(MT // 2, MT):
-            e_tile(m)
+        for m in range(MT + LEAD):
+            if m >= LEAD:
+                e_tile(m - LEAD)
+            if m < MT:
+                f_tile(m)

@@ -202,8 +202,8 @@ def tile_list_turnout_companions_kernel(tc, tab_words, tab_scales, offs, offs2, 
                 for u in range(2):
                     cast = nc.vector.tensor_copy if (b, u) == (1, 1) else nc.scalar.copy
                     cast(
-                        out=grouped[:].rearrange("p (t m j) -> p m j t", t=SLOTS, j=SLOTS)[:, 64 * u : 64 * (u + 1)],
-                        in_=w1_raw[a, b].rearrange("p (j m t) -> p m j t", t=SLOTS, j=SLOTS)[:, 64 * u : 64 * (u + 1)])
+                        out=grouped[:].rearrange("p (g t m j) -> p g m j t", g=2, t=2, j=SLOTS)[:, :, 64 * u : 64 * (u + 1)],
+                        in_=w1_raw[a, b].rearrange("p (j m g t) -> p g m j t", g=2, t=2, j=SLOTS)[:, :, 64 * u : 64 * (u + 1)])
                 codes = held("w1_w%d%d" % (a, b), [P, 512], U32)
                 scales = held("w1_sc%d%d" % (a, b), [P, 512], U8)
                 nc.vector.quantize_mx(out=codes[:].bitcast(FP8X4), scales=scales[:], in_=grouped[:])

@@ -24,8 +24,8 @@ NCH = S // CH
 MT = S2 // P
 RES_SLICE = 512
 LEAD = 5
-HI = 2 * 8192
-LO = HI + 4096
+WF = 4 * 8192 + 128
+LATE = WF + 4096 + 512 + 128
 
 
 def tile_list_turnout_companions_kernel(tc, tab_words, tab_scales, offs, offs2, w1, w4_words, w4_scales,
@@ -43,55 +43,52 @@ def tile_list_turnout_companions_kernel(tc, tab_words, tab_scales, offs, offs2, 
         offs_sb = keep.tile([P, S // 16], U16, name="offs_sb")
         offs2_sb = keep.tile([P, S2 // 16], U16, name="offs2_sb")
         tab_sc = held("tab_sc", [P, T], U8)
-        w4_raw = held("w4_raw", [P, PASSES * 2 * K], U8)
-        wf_sc = held("wf_sc", [P, S], U8)
         v_sc1 = held("v_sc1", [P, S], U8)
-        warm_in = shared.tile([P, 32], F32, name="warm_in", align_bytes=64, offset=LO + 16384 - 64)
-        warm_out = shared.tile([P, 192], F32, name="warm_out", align_bytes=64, offset=HI + 1920)
+        zero_bias = held("zero_bias", [P, 8], F32)
 
+        def staged(name, shape, dtype, offset):
+            return shared.tile(shape, dtype, name=name, align_bytes=64, offset=offset)
+
+        w4_sc_raw = staged("w4_sc_raw", [P, PASSES * K], U8, LATE)
+        zeros_a = held("zeros_a", [P, 8], F32)
+        zeros_b = held("zeros_b", [P, 8], F32)
+        zeros_c = held("zeros_c", [P, 8], F32)
+        w4_region = staged("w4_raw", [P, LATE], U8, 0)
+        w4_raw = w4_region[:, 0 : PASSES * 2 * K]
+
+        nc.vector.memset(zeros_a[:], 0.0)
         nc.vector.memset(tab_sc[:].bitcast(I32), 0)
-        nc.vector.memset(warm_in[:], 0.0)
-        nc.gpsimd.memset(v_sc1[:].bitcast(I32), 0)
+        nc.vector.tensor_copy(zeros_b[:], zeros_a[:])
+        nc.vector.memset(w4_sc_raw[:, 0 : 2 * K].bitcast(I32), 0)
+        nc.vector.tensor_copy(zeros_c[:, 0:8], zeros_b[:])
+        nc.vector.memset(v_sc1[:].bitcast(I32), 0)
+        nc.scalar.activation(zero_bias[:], zeros_c[:, 0:8], ACT.Gelu_apprx_tanh)
 
-        nc.sync.dma_start(offs_sb[:], offs)
-        for q in range(4):
-            nc.scalar.dma_start(out=tab_sc[32 * q : 32 * q + 8, :].bitcast(I32),
-                                in_=tab_scales[:, 4 * q : 4 * q + 4, :].bitcast(I32))
-        nc.scalar.activation(warm_out[:, 0:32], warm_in[:], ACT.Gelu_apprx_tanh)
-        nc.gpsimd.memset(wf_sc[:].bitcast(I32), 0)
-        for q in range(4):
-            nc.gpsimd.dma_start(out=wf_sc[32 * q : 32 * q + 8, :].bitcast(I32),
-                                in_=wf_scales[:, 4 * q : 4 * q + 4, :].bitcast(I32))
-
-        tab_w = [held("tab_w0", [P, T], U32), shared.tile([P, T], U32, name="tab_w1", align_bytes=64, offset=LO + 16384)]
-        w1_lo = shared.tile([P, 2 * 2048], F32, name="w1_lo", align_bytes=64, offset=LO)
-        w1_raw = {(a, 0): w1_lo[:, 2048 * a : 2048 * (a + 1)] for a in range(PASSES)}
-        gain_sb = shared.tile([P, PASSES * SLOTS], F32, name="gain_sb", align_bytes=64, offset=HI + 2560)
+        tab_w = [held("tab_w0", [P, T], U32, tag="zeros_a")]
+        w1_raw = {(0, 0): held("w1_raw00", [P, 2048], F32, tag="zeros_b")}
 
         def load_w1(a, b, u, width):
             c0 = 512 * b + width * u
             nc.sync.dma_start(
-                out=w1_raw[a, b].rearrange("p (j c) -> p j c", j=SLOTS)[:, :, width * u : width * (u + 1)],
+                out=w1_raw[a, b][:].rearrange("p (j c) -> p j c", j=SLOTS)[:, :, width * u : width * (u + 1)],
                 in_=w1[512 * a : 512 * (a + 1), c0 : c0 + width].rearrange("(p j) c -> p j c", j=SLOTS))
 
         def load_tab(a):
             nc.sync.dma_start(out=tab_w[a][:].bitcast(I32),
                               in_=tab_words[a].rearrange("p t i -> p (t i)").bitcast(I32))
 
-        nc.sync.dma_start(out=w4_raw[:].bitcast(I32).rearrange("p (a c) -> p a c", a=PASSES),
-                          in_=w4_words.bitcast(I32).rearrange("a p c -> p a c"))
-        load_tab(0)
+        nc.sync.dma_start(offs_sb[:], offs)
         nc.sync.dma_start(offs2_sb[:], offs2)
-        load_tab(1)
-        load_w1(0, 0, 0, 512)
-        load_w1(1, 0, 0, 512)
-        nc.sync.dma_start(out=gain_sb[:].rearrange("p (b t) -> p b t", t=SLOTS),
-                          in_=gain.rearrange("(b p t) -> p b t", p=P, t=SLOTS))
-        w4_sc_raw = shared.tile([P, PASSES * K], U8, name="w4_sc_raw", align_bytes=64, offset=HI - 64)
-        nc.vector.memset(w4_sc_raw[:].bitcast(I32), 0)
+        nc.sync.dma_start(out=w4_raw.bitcast(I32).rearrange("p (a c) -> p a c", a=PASSES),
+                          in_=w4_words.bitcast(I32).rearrange("a p c -> p a c"))
         for q in range(4):
-            nc.scalar.dma_start(out=w4_sc_raw[32 * q : 32 * q + 4, :].bitcast(I32),
-                                in_=w4_scales[:, 4 * q : 4 * q + 4, :].bitcast(I32).rearrange("a r c -> r a c"))
+            nc.sync.dma_start(out=tab_sc[32 * q : 32 * q + 8, :].bitcast(I32),
+                              in_=tab_scales[:, 4 * q : 4 * q + 4, :].bitcast(I32))
+        load_tab(0)
+        for q in range(4):
+            nc.sync.dma_start(out=w4_sc_raw[32 * q : 32 * q + 4, 0 : 2 * K].bitcast(I32),
+                              in_=w4_scales[:, 4 * q : 4 * q + 4, :].bitcast(I32).rearrange("a r c -> r a c"))
+        load_w1(0, 0, 0, 512)
 
         v_sc = held("v_sc", [P, S], U8)
         v_w = [held("v_w%d" % a, [P, S], U32) for a in range(PASSES)]
@@ -110,24 +107,39 @@ def tile_list_turnout_companions_kernel(tc, tab_words, tab_scales, offs, offs2, 
 
         nc.vector.tensor_copy(v_sc[:], tab_sc[:].indirect(offs_sb[:]))
         for q in range(4):
-            nc.gpsimd.dma_start(out=v_sc1[32 * q : 32 * q + 4, :].bitcast(I32),
-                                in_=v_sc[32 * q + 4 : 32 * q + 8, :].bitcast(I32))
+            nc.sync.dma_start(out=v_sc1[32 * q : 32 * q + 4, :].bitcast(I32),
+                              in_=v_sc[32 * q + 4 : 32 * q + 8, :].bitcast(I32))
         deal_words(0)
+        deal_words(1)
         nc.vector.tensor_copy(v_w[0][:], tab_w[0][:].indirect(offs_sb[:]))
         deal_scales(0)
-        nc.vector.tensor_copy(v_w[1][:], tab_w[1][:].indirect(offs_sb[:]))
-        deal_words(1)
         deal_scales(1)
 
-        wf_w = held("wf_w", [P, PASSES * S], U32, tag="w4_raw")
+        tab_w.append(staged("tab_w1", [P, T], U32, 0))
+        for i, (a, b) in enumerate(((1, 0), (0, 1), (1, 1))):
+            w1_raw[a, b] = staged("w1_raw%d%d" % (a, b), [P, 2048], F32, 8192 * (i + 1))
+        wf_w = staged("wf_w", [P, PASSES * S], U32, WF)
+        wf_sc = staged("wf_sc", [P, S], U8, WF + 4096)
+        gain_sb = staged("gain_sb", [P, PASSES * SLOTS], F32, WF + 4096 + 512)
+        gv_sb = staged("gv_sb", [P, MT], F32, WF + 4096 + 512 + 64)
+        nc.vector.memset(wf_sc[:].bitcast(I32), 0)
+
+        load_tab(1)
+        nc.sync.dma_start(out=gain_sb[:].rearrange("p (b t) -> p b t", t=SLOTS),
+                          in_=gain.rearrange("(b p t) -> p b t", p=P, t=SLOTS))
+        load_w1(1, 0, 0, 512)
         nc.sync.dma_start(out=wf_w[:].bitcast(I32).rearrange("p (a c) -> p a c", a=PASSES),
                           in_=wf_words.rearrange("a p c i -> p a (c i)").bitcast(I32))
-        w1_hi = shared.tile([P, 2 * 2048], F32, name="w1_hi", align_bytes=64, offset=0)
-        for a in range(PASSES):
-            w1_raw[a, 1] = w1_hi[:, 2048 * a : 2048 * (a + 1)]
+        for q in range(4):
+            nc.sync.dma_start(out=wf_sc[32 * q : 32 * q + 8, :].bitcast(I32),
+                              in_=wf_scales[:, 4 * q : 4 * q + 4, :].bitcast(I32))
         load_w1(0, 1, 0, 512)
         load_w1(1, 1, 0, 256)
         load_w1(1, 1, 1, 256)
+        with nc.allow_non_contiguous_dma(reason="one factor a partition"):
+            nc.sync.dma_start(out=gv_sb[:], in_=gv.rearrange("(mt p) -> p mt", p=P))
+
+        nc.vector.tensor_copy(v_w[1][:], tab_w[1][:].indirect(offs_sb[:]))
 
         r_sc = {}
         r_w = {}
@@ -191,24 +203,27 @@ def tile_list_turnout_companions_kernel(tc, tab_words, tab_scales, offs, offs2, 
             return quantize_halves("bq%d" % b, grouped)
 
         bq = [b_block_scalar(0), b_block_vector(1)]
-        gv_sb = held("gv_sb", [P, MT], F32, tag="w4_w0")
-        with nc.allow_non_contiguous_dma(reason="one factor a partition"):
-            nc.sync.dma_start(out=gv_sb[:], in_=gv.rearrange("(mt p) -> p mt", p=P))
 
         def h_block(b):
             w1q = []
             for a in range(PASSES):
-                grouped = held("w1_g%d%d" % (a, b), [P, 2048], BF16)
+                if (a, b) == (1, 1):
+                    grouped = staged("w1_g11", [P, 2048], BF16, LATE + 4096)
+                else:
+                    grouped = held("w1_g%d%d" % (a, b), [P, 2048], BF16)
                 for u in range(2):
-                    cast = nc.vector.tensor_copy if (b, u) == (1, 1) else nc.scalar.copy
+                    cast = nc.vector.tensor_copy if (a, b, u) == (1, 1, 1) else nc.scalar.copy
                     cast(
                         out=grouped[:].rearrange("p (g t m j) -> p g m j t", g=2, t=2, j=SLOTS)[:, :, 64 * u : 64 * (u + 1)],
-                        in_=w1_raw[a, b].rearrange("p (j m g t) -> p g m j t", g=2, t=2, j=SLOTS)[:, :, 64 * u : 64 * (u + 1)])
+                        in_=w1_raw[a, b][:].rearrange("p (j m g t) -> p g m j t", g=2, t=2, j=SLOTS)[:, :, 64 * u : 64 * (u + 1)])
                 codes = held("w1_w%d%d" % (a, b), [P, 512], U32)
                 scales = held("w1_sc%d%d" % (a, b), [P, 512], U8)
                 nc.vector.quantize_mx(out=codes[:].bitcast(FP8X4), scales=scales[:], in_=grouped[:])
                 w1q.append((codes, scales))
-            grouped = held("h_g%d" % b, [P, S * SLOTS], BF16)
+            if b == 0:
+                grouped = staged("h_g0", [P, S * SLOTS], BF16, 3 * 8192 - 4096 + 64)
+            else:
+                grouped = held("h_g1", [P, S * SLOTS], BF16)
             for c in range(NCH):
                 bank = psum.tile([P, SLOTS, CH], F32, name="first", tag="first")
                 for a in range(PASSES):
@@ -241,28 +256,35 @@ def tile_list_turnout_companions_kernel(tc, tab_words, tab_scales, offs, offs2, 
                 resident_pass(bank, m, a, wf_w[:, S * a : S * (a + 1)], wf_sc[4 * a : P, :], a == 0, False)
             for a in range(PASSES):
                 resident_pass(bank, m, a, bq[a][0][:], bq[a][1][:], False, a == PASSES - 1)
-            f_m = held("f_sb%d" % m, [P, S], F32)
-            nc.scalar.copy(out=f_m[:], in_=bank[:])
+            if m < 4:
+                f_m = staged("f_sb%d" % m, [P, S], F32, 3 * 8192 + 64 + 2048 * m)
+            else:
+                f_m = held("f_sb%d" % m, [P, S], F32)
+            if m == 4:
+                nc.vector.tensor_copy(out=f_m[:], in_=bank[:])
+            else:
+                nc.scalar.copy(out=f_m[:], in_=bank[:])
             f_sb.append(f_m)
 
         def e_tile(m):
-            bank = psum.tile([P, S], F32, name="second", tag="second")
+            bank = psum.tile([P, S], F32, name="first", tag="first")
             for a in range(PASSES):
                 resident_pass(bank, m, a, hq[a][0][:], hq[a][1][:], a == 0, a == PASSES - 1)
             larger = ring.tile([P, S], F32, name="larger")
             nc.vector.scalar_tensor_tensor(out=larger[:], in0=bank[:], scalar=gv_sb[:, m : m + 1], in1=f_sb[m][:],
                                            op0=ALU.mult, op1=ALU.max)
-            result = ring.tile([P, S], F32, name="result")
-            nc.scalar.activation(out=result[:], in_=larger[:], func=ACT.Gelu_apprx_tanh)
+            result = held("result%d" % m, [P, S], F32)
+            nc.scalar.activation(out=result[:], in_=larger[:], func=ACT.Gelu_apprx_tanh,
+                                 bias=zero_bias[:, 0:1])
             nc.sync.dma_start(out=out[P * m : P * (m + 1), :], in_=result[:])
 
         hq = [h_block(0), h_block(1)]
-        gather_residents(0, shared.tile([P, RES_SLICE], U8, name="r_sc0", align_bytes=64, offset=HI),
-                         [shared.tile([P, RES_SLICE], U32, name="r_w00", align_bytes=64, offset=HI + 512),
-                          held("r_w10", [P, RES_SLICE], U32)])
-        gather_residents(1, held("r_sc1", [P, RES_SLICE], U8, tag="w1_g10"),
-                         [held("r_w01", [P, RES_SLICE], U32, tag="w1_g01"),
-                          held("r_w11", [P, RES_SLICE], U32, tag="w1_g11")])
+        gather_residents(0, staged("r_sc0", [P, RES_SLICE], U8, LATE),
+                         [staged("r_w00", [P, RES_SLICE], U32, LATE + 512),
+                          held("r_w10", [P, RES_SLICE], U32, tag="w1_g00")])
+        gather_residents(1, staged("r_sc1", [P, RES_SLICE], U8, LATE + 4096),
+                         [staged("r_w01", [P, RES_SLICE], U32, LATE + 4096 + 512),
+                          staged("r_w11", [P, RES_SLICE], U32, LATE + 4096 + 2560)])
         for m in range(MT + LEAD):
             if m >= LEAD:
                 e_tile(m - LEAD)

from contextlib import ExitStack

import concourse.mybir as mybir

K, T, S, S2 = 1024, 2048, 512, 1024
FLOPS = 2 * K * K * S * 2 + 2 * K * S2 * S * 3

F32 = mybir.dt.float32
BF16 = mybir.dt.bfloat16
I32 = mybir.dt.int32
U32 = mybir.dt.uint32
U16 = mybir.dt.uint16
U8 = mybir.dt.uint8
FP8X4 = mybir.dt.float8_e4m3fn_x4
FP4X4 = mybir.dt.float4_e2m1fn_x4
ACT = mybir.ActivationFunctionType
ALU = mybir.AluOpType

P = 128
PASSES = 2
SLOTS = 4
CH = 128
NCH = S // CH
MT = S2 // P
RES_SLICE = 512
LEAD = 5
WF = 4 * 8192 + 128
LATE = WF + 4096 + 512 + 128


def tile_list_turnout_companions_kernel(tc, tab_words, tab_scales, offs, offs2, w1, w4_words, w4_scales,
                                                  wf_words, wf_scales, gain, gv, out):
    nc = tc.nc
    with ExitStack() as ctx:
        keep = ctx.enter_context(tc.tile_pool(name="keep", bufs=1))
        ring = ctx.enter_context(tc.tile_pool(name="ring", bufs=4))
        shared = ctx.enter_context(tc.tile_pool(name="shared", bufs=1))
        psum = ctx.enter_context(tc.psum_pool(name="psum", bufs=4))

        def held(name, shape, dtype, tag=""):
            return keep.tile(shape, dtype, name=name, tag=tag or name, align_bytes=64)

        offs_sb = keep.tile([P, S // 16], U16, name="offs_sb")
        offs2_sb = keep.tile([P, S2 // 16], U16, name="offs2_sb")
        tab_sc = held("tab_sc", [P, T], U8)
        v_sc1 = held("v_sc1", [P, S], U8)
        zero_bias = held("zero_bias", [P, 8], F32)

        def staged(name, shape, dtype, offset):
            return shared.tile(shape, dtype, name=name, align_bytes=64, offset=offset)

        w4_sc_raw = staged("w4_sc_raw", [P, PASSES * K], U8, LATE)
        zeros_a = held("zeros_a", [P, 8], F32)
        zeros_b = held("zeros_b", [P, 8], F32)
        zeros_c = held("zeros_c", [P, 8], F32)
        w4_region = staged("w4_raw", [P, LATE], U8, 0)
        w4_raw = w4_region[:, 0 : PASSES * 2 * K]

        nc.vector.memset(zeros_a[:], 0.0)
        nc.vector.memset(tab_sc[:].bitcast(I32), 0)
        nc.vector.tensor_copy(zeros_b[:], zeros_a[:])
        nc.vector.memset(w4_sc_raw[:, 0 : 2 * K].bitcast(I32), 0)
        nc.vector.tensor_copy(zeros_c[:, 0:8], zeros_b[:])
        nc.vector.memset(v_sc1[:].bitcast(I32), 0)
        nc.scalar.activation(zero_bias[:], zeros_c[:, 0:8], ACT.Gelu_apprx_tanh)

        tab_w = [held("tab_w0", [P, T], U32, tag="zeros_a")]
        w1_raw = {(0, 0): held("w1_raw00", [P, 2048], F32, tag="zeros_b")}

        def load_w1(a, b, u, width):
            c0 = 512 * b + width * u
            nc.sync.dma_start(
                out=w1_raw[a, b][:].rearrange("p (j c) -> p j c", j=SLOTS)[:, :, width * u : width * (u + 1)],
                in_=w1[512 * a : 512 * (a + 1), c0 : c0 + width].rearrange("(p j) c -> p j c", j=SLOTS))

        def load_tab(a):
            nc.sync.dma_start(out=tab_w[a][:].bitcast(I32),
                              in_=tab_words[a].rearrange("p t i -> p (t i)").bitcast(I32))

        nc.sync.dma_start(offs_sb[:], offs)
        nc.sync.dma_start(offs2_sb[:], offs2)
        nc.sync.dma_start(out=w4_raw.bitcast(I32).rearrange("p (a c) -> p a c", a=PASSES),
                          in_=w4_words.bitcast(I32).rearrange("a p c -> p a c"))
        for q in range(4):
            nc.sync.dma_start(out=tab_sc[32 * q : 32 * q + 8, :].bitcast(I32),
                              in_=tab_scales[:, 4 * q : 4 * q + 4, :].bitcast(I32))
        load_tab(0)
        for q in range(4):
            nc.sync.dma_start(out=w4_sc_raw[32 * q : 32 * q + 4, 0 : 2 * K].bitcast(I32),
                              in_=w4_scales[:, 4 * q : 4 * q + 4, :].bitcast(I32).rearrange("a r c -> r a c"))
        load_w1(0, 0, 0, 512)

        v_sc = held("v_sc", [P, S], U8)
        v_w = [held("v_w%d" % a, [P, S], U32) for a in range(PASSES)]
        w4_w = [held("w4_w%d" % a, [P, 2 * K], U8) for a in range(PASSES)]
        w4_sc = held("w4_sc", [P, PASSES * K], U8)

        def deal_words(a):
            nc.vector.tensor_copy(
                out=w4_w[a][:].bitcast(U16).rearrange("p (t o i) -> p o t i", t=SLOTS, i=8),
                in_=w4_raw[:, 2 * K * a : 2 * K * (a + 1)].bitcast(U16).rearrange("p (o i t) -> p o t i", t=SLOTS, i=8))

        def deal_scales(a):
            nc.vector.tensor_copy(
                out=w4_sc[:, K * a : K * (a + 1)].rearrange("p (t o i) -> p o t i", t=SLOTS, i=16),
                in_=w4_sc_raw[:, K * a : K * (a + 1)].rearrange("p (o i t) -> p o t i", t=SLOTS, i=16))

        nc.vector.tensor_copy(v_sc[:], tab_sc[:].indirect(offs_sb[:]))
        for q in range(4):
            nc.sync.dma_start(out=v_sc1[32 * q : 32 * q + 4, :].bitcast(I32),
                              in_=v_sc[32 * q + 4 : 32 * q + 8, :].bitcast(I32))
        deal_words(0)
        deal_words(1)
        nc.vector.tensor_copy(v_w[0][:], tab_w[0][:].indirect(offs_sb[:]))
        deal_scales(0)
        deal_scales(1)

        tab_w.append(staged("tab_w1", [P, T], U32, 0))
        for i, (a, b) in enumerate(((1, 0), (0, 1), (1, 1))):
            w1_raw[a, b] = staged("w1_raw%d%d" % (a, b), [P, 2048], F32, 8192 * (i + 1))
        wf_w = staged("wf_w", [P, PASSES * S], U32, WF)
        wf_sc = staged("wf_sc", [P, S], U8, WF + 4096)
        gain_sb = staged("gain_sb", [P, PASSES * SLOTS], F32, WF + 4096 + 512)
        gv_sb = staged("gv_sb", [P, MT], F32, WF + 4096 + 512 + 64)
        nc.vector.memset(wf_sc[:].bitcast(I32), 0)

        load_tab(1)
        nc.sync.dma_start(out=gain_sb[:].rearrange("p (b t) -> p b t", t=SLOTS),
                          in_=gain.rearrange("(b p t) -> p b t", p=P, t=SLOTS))
        load_w1(1, 0, 0, 512)
        nc.sync.dma_start(out=wf_w[:].bitcast(I32).rearrange("p (a c) -> p a c", a=PASSES),
                          in_=wf_words.rearrange("a p c i -> p a (c i)").bitcast(I32))
        for q in range(4):
            nc.sync.dma_start(out=wf_sc[32 * q : 32 * q + 8, :].bitcast(I32),
                              in_=wf_scales[:, 4 * q : 4 * q + 4, :].bitcast(I32))
        load_w1(0, 1, 0, 512)
        load_w1(1, 1, 0, 256)
        load_w1(1, 1, 1, 256)
        with nc.allow_non_contiguous_dma(reason="one factor a partition"):
            nc.sync.dma_start(out=gv_sb[:], in_=gv.rearrange("(mt p) -> p mt", p=P))

        nc.vector.tensor_copy(v_w[1][:], tab_w[1][:].indirect(offs_sb[:]))

        r_sc = {}
        r_w = {}

        def gather_residents(s, scales, words):
            cols = offs2_sb[:, s * RES_SLICE // 16 : (s + 1) * RES_SLICE // 16]
            r_sc[s] = scales
            nc.vector.tensor_copy(r_sc[s][:], tab_sc[:].indirect(cols))
            for a in range(PASSES):
                r_w[a, s] = words[a]
                nc.vector.tensor_copy(r_w[a, s][:], tab_w[a][:].indirect(cols))

        def quantize_halves(name, grouped):
            codes = held(name + "_w", [P, S], U32)
            scales = held(name + "_sc", [P, S], U8)
            for u in range(2):
                nc.vector.quantize_mx(out=codes[:, 256 * u : 256 * (u + 1)].bitcast(FP8X4),
                                      scales=scales[:, 256 * u : 256 * (u + 1)],
                                      in_=grouped[:, 1024 * u : 1024 * (u + 1)])
            return codes, scales

        def w4_pass(dst, a, b, t, cols, start, stop):
            col = 256 * t + P * b
            plane = v_sc if a == 0 else v_sc1
            nc.tensor.matmul_mx(
                out=dst,
                lhsT=w4_w[a][:, 2 * col : 2 * (col + P)].bitcast(FP4X4),
                lhsT_scale=w4_sc[:, K * a + col : K * a + col + P],
                rhs=v_w[a][:, cols].bitcast(FP8X4), rhs_scale=plane[:, cols], start=start, stop=stop)

        def b_block_vector(b):
            grouped = held("b_g%d" % b, [P, S * SLOTS], BF16)
            banks = [psum.tile([P, SLOTS, CH], F32, name="second", tag="second") for c in range(NCH)]
            for a in range(PASSES):
                for c in range(NCH):
                    for t in range(SLOTS):
                        w4_pass(banks[c][:, t, :], a, b, t, slice(CH * c, CH * (c + 1)),
                                a == 0 and t == 0, a == PASSES - 1 and t == SLOTS - 1)
            for c in range(NCH):
                nc.vector.tensor_tensor(
                    out=grouped[:, SLOTS * CH * c : SLOTS * CH * (c + 1)].rearrange("p (n t) -> p n t", t=SLOTS),
                    in0=banks[c][:].rearrange("p t n -> p n t"),
                    in1=gain_sb[:, SLOTS * b : SLOTS * (b + 1)].unsqueeze(1).to_broadcast([P, CH, SLOTS]),
                    op=ALU.mult)
            return quantize_halves("bq%d" % b, grouped)

        def b_block_scalar(b):
            flat = held("b_flat%d" % b, [P, SLOTS * S], BF16)
            grouped = held("b_g%d" % b, [P, S * SLOTS], BF16)
            banks = [psum.tile([P, S], F32, name="first", tag="first") for t in range(SLOTS)]
            for a in range(PASSES):
                for t in range(SLOTS):
                    w4_pass(banks[t][:], a, b, t, slice(0, S), a == 0, a == PASSES - 1)
            for t in range(SLOTS):
                nc.scalar.activation(out=flat[:, S * t : S * (t + 1)], in_=banks[t][:], func=ACT.Copy,
                                     scale=gain_sb[:, SLOTS * b + t : SLOTS * b + t + 1])
            for u in range(2):
                nc.vector.tensor_copy(
                    out=grouped[:, 1024 * u : 1024 * (u + 1)].rearrange("p (c i t) -> p c t i", t=SLOTS, i=4),
                    in_=flat[:].rearrange("p (t c i) -> p c t i", t=SLOTS, i=4)[:, 64 * u : 64 * (u + 1)])
            return quantize_halves("bq%d" % b, grouped)

        bq = [b_block_scalar(0), b_block_vector(1)]

        def h_block(b):
            w1q = []
            for a in range(PASSES):
                if (a, b) == (1, 1):
                    grouped = staged("w1_g11", [P, 2048], BF16, LATE + 4096)
                else:
                    grouped = held("w1_g%d%d" % (a, b), [P, 2048], BF16)
                for u in range(2):
                    cast = nc.vector.tensor_copy if (a, b, u) == (1, 1, 1) else nc.scalar.copy
                    cast(
                        out=grouped[:].rearrange("p (g t m j) -> p g m j t", g=2, t=2, j=SLOTS)[:, :, 64 * u : 64 * (u + 1)],
                        in_=w1_raw[a, b][:].rearrange("p (j m g t) -> p g m j t", g=2, t=2, j=SLOTS)[:, :, 64 * u : 64 * (u + 1)])
                codes = held("w1_w%d%d" % (a, b), [P, 512], U32)
                scales = held("w1_sc%d%d" % (a, b), [P, 512], U8)
                nc.vector.quantize_mx(out=codes[:].bitcast(FP8X4), scales=scales[:], in_=grouped[:])
                w1q.append((codes, scales))
            if b == 0:
                grouped = staged("h_g0", [P, S * SLOTS], BF16, 3 * 8192 - 4096 + 64)
            else:
                grouped = held("h_g1", [P, S * SLOTS], BF16)
            for c in range(NCH):
                bank = psum.tile([P, SLOTS, CH], F32, name="first", tag="first")
                for a in range(PASSES):
                    for t in range(SLOTS):
                        nc.tensor.matmul_mx(
                            out=bank[:, t, :],
                            lhsT=w1q[a][0][:, P * t : P * (t + 1)].bitcast(FP8X4),
                            lhsT_scale=w1q[a][1][:, P * t : P * (t + 1)],
                            rhs=v_w[a][:, CH * c : CH * (c + 1)].bitcast(FP8X4),
                            rhs_scale=v_sc[4 * a : P, CH * c : CH * (c + 1)],
                            start=(a == 0 and t == 0), stop=(a == PASSES - 1 and t == SLOTS - 1))
                nc.scalar.activation(
                    out=grouped[:, SLOTS * CH * c : SLOTS * CH * (c + 1)].rearrange("p (n t) -> p n t", t=SLOTS),
                    in_=bank[:].rearrange("p t n -> p n t"), func=ACT.Abs)
            return quantize_halves("hq%d" % b, grouped)

        def resident_pass(bank, m, a, codes, scales, start, stop):
            s, c0 = divmod(P * m, RES_SLICE)
            nc.tensor.matmul_mx(
                out=bank[:],
                lhsT=r_w[a, s][:, c0 : c0 + P].bitcast(FP8X4),
                lhsT_scale=r_sc[s][4 * a : P, c0 : c0 + P],
                rhs=codes.bitcast(FP8X4), rhs_scale=scales, start=start, stop=stop)

        f_sb = []

        def f_tile(m):
            bank = psum.tile([P, S], F32, name="second", tag="second")
            for a in range(PASSES):
                resident_pass(bank, m, a, wf_w[:, S * a : S * (a + 1)], wf_sc[4 * a : P, :], a == 0, False)
            for a in range(PASSES):
                resident_pass(bank, m, a, bq[a][0][:], bq[a][1][:], False, a == PASSES - 1)
            if m < 4:
                f_m = staged("f_sb%d" % m, [P, S], F32, 3 * 8192 + 64 + 2048 * m)
            else:
                f_m = held("f_sb%d" % m, [P, S], F32)
            if m == 4:
                nc.vector.tensor_copy(out=f_m[:], in_=bank[:])
            else:
                nc.scalar.copy(out=f_m[:], in_=bank[:])
            f_sb.append(f_m)

        def e_tile(m):
            bank = psum.tile([P, S], F32, name="first", tag="first")
            for a in range(PASSES):
                resident_pass(bank, m, a, hq[a][0][:], hq[a][1][:], a == 0, a == PASSES - 1)
            larger = ring.tile([P, S], F32, name="larger")
            nc.vector.scalar_tensor_tensor(out=larger[:], in0=bank[:], scalar=gv_sb[:, m : m + 1], in1=f_sb[m][:],
                                           op0=ALU.mult, op1=ALU.max)
            result = held("result%d" % m, [P, S], F32)
            nc.scalar.activation(out=result[:], in_=larger[:], func=ACT.Gelu_apprx_tanh,
                                 bias=zero_bias[:, 0:1])
            nc.sync.dma_start(out=out[P * m : P * (m + 1), :], in_=result[:])

        hq = [h_block(0), h_block(1)]
        gather_residents(0, staged("r_sc0", [P, RES_SLICE], U8, LATE),
                         [staged("r_w00", [P, RES_SLICE], U32, LATE + 512),
                          held("r_w10", [P, RES_SLICE], U32, tag="w1_g00")])
        gather_residents(1, staged("r_sc1", [P, RES_SLICE], U8, LATE + 4096),
                         [staged("r_w01", [P, RES_SLICE], U32, LATE + 4096 + 512),
                          staged("r_w11", [P, RES_SLICE], U32, LATE + 4096 + 2560)])
        for m in range(MT + LEAD):
            if m >= LEAD:
                e_tile(m - LEAD)
            if m < MT:
                f_tile(m)
